import numpy as np
import ml_dtypes


def mxq(x, axis, fmt="e4m3"):
    dtype, down = {"e4m3": (ml_dtypes.float8_e4m3fn, 7), "e5m2": (ml_dtypes.float8_e5m2, 14)}[fmt]
    v = np.moveaxis(np.asarray(x, np.float32).astype(ml_dtypes.bfloat16).astype(np.float64), axis, -1)
    blocks = v.reshape(v.shape[:-1] + (-1, 32))
    amax = np.abs(blocks).max(-1, keepdims=True)
    byte = np.maximum(np.where(amax > 0, np.frexp(amax)[1] - 1 + 127, 0) - down, 1)
    scale = np.exp2(byte - 127.0)
    codes = (blocks / scale).astype(np.float32).astype(dtype).astype(np.float64)
    return np.moveaxis((codes * scale).reshape(v.shape), -1, axis)


WIDE = False


def mx_kscale(k):
    if not WIDE:
        return np.ones(k)
    levels = np.array([10, -10, 5, -5, 0])
    if k % 512:
        return np.exp2(np.random.permutation(np.resize(levels, k // 32))).repeat(32)
    a = np.empty((k // 512, 16))
    for p in range(k // 512):
        a[p, :8] = np.random.permutation(np.resize(levels, 8))
        for g in range(8):
            far = levels[np.abs(levels - a[p, g]) >= 10]
            a[p, g + 8] = far[np.random.randint(len(far))]
    return np.exp2(a.ravel()).repeat(32)


def f64(x):
    return np.asarray(x).astype(np.float64)


def striped(idx):
    return np.tile(np.asarray(idx).reshape(-1, 16).T, (8, 1)).astype(np.uint16)


def unstriped(offs):
    return offs[:16].T.reshape(-1).astype(np.int64)


B, N, C, D, NQ = 1, 512, 2048, 512, 256
SEG = 32


def eight(codes):
    return np.concatenate([codes[h].reshape(-1, 16).T for h in range(8)]).astype(np.uint16)


def uneight(offs):
    return np.stack([offs[16 * h:16 * h + 16].T.reshape(-1) for h in range(8)]).astype(np.int64)


def setup_inputs():
    n = np.random.standard_normal
    s = mx_kscale(D)[:, None]
    grid = lambda x: np.round(x * 32) / 32
    return {
        "qT": (n((B, D, NQ)) * s / np.sqrt(D)).astype(np.float32),
        "cb": (grid(n((D, C))) / s).astype(np.float32),
        "norm": np.tile(np.random.randint(32, 129, N) / 64.0, (128, 1)).astype(np.float32),
        "offs": eight(np.random.randint(0, C, (8, N))),
    }


def reference(qT, cb, norm, offs):
    k = []
    for part, offs_ in enumerate((offs,)):
        codes = uneight(offs_)
        k += [f64(cb)[512 * part + 64 * h:512 * part + 64 * h + 64][:, codes[h]] for h in range(8)]
    k = np.concatenate(k) * f64(norm)[:1]
    a = mxq(f64(qT), 1, "e4m3").transpose(0, 2, 1) @ mxq(k, 0, "e4m3")
    return a.reshape(B, NQ, N // SEG, SEG).max(-1)

@@ -1,0 +1,134 @@
+from contextlib import ExitStack
+
+import concourse.mybir as mybir
+from concourse.masks import make_identity
+
+F32 = mybir.dt.float32
+BF16 = mybir.dt.bfloat16
+U32 = mybir.dt.uint32
+U16 = mybir.dt.uint16
+U8 = mybir.dt.uint8
+FP8X4 = mybir.dt.float8_e4m3fn_x4
+MULT = mybir.AluOpType.mult
+MAX = mybir.AluOpType.max
+AXIS_X = mybir.AxisListType.X
+
+D, C, N, NQ, SEG = 512, 2048, 512, 256, 32
+P = 128
+FLOPS = 2 * D * N * NQ
+
+SLICES = ((0, 128), (128, 128), (256, 128), (384, 128))
+
+
+def tile_attend_pq_max32_kernel(tc, qT, cb, norm, offs, out):
+    nc = tc.nc
+    with ExitStack() as ctx:
+        held = ctx.enter_context(tc.tile_pool(name="held", bufs=1))
+        psum = ctx.enter_context(tc.psum_pool(name="psum", bufs=1))
+
+        offsets = held.tile([P, N // 16], U16, name="offsets")
+        norm4 = held.tile([P, 4], F32, name="norm4")
+        planes = [held.tile([P, C], F32, name=f"plane{t}") for t in range(4)]
+        q_raw = held.tile([P, 4, NQ], F32, name="q_raw")
+
+        cb_rows = cb.rearrange("(p t) c -> p t c", t=4)
+        nc.sync.dma_start(planes[0][:], cb_rows[:, 0, :])
+        nc.sync.dma_start(norm4[:], norm[0:1, :].rearrange("o (p b) -> (o p) b", b=4))
+        nc.sync.dma_start(offsets[:], offs)
+        for t in range(1, 4):
+            nc.sync.dma_start(planes[t][:], cb_rows[:, t, :])
+        nc.sync.dma_start(q_raw[:], qT[0].rearrange("(p t) q -> p t q", t=4))
+
+        ident = held.tile([P, P], F32, name="ident")
+        make_identity(nc, ident[:])
+
+        norm_ps = psum.tile([P, 4, P], F32, name="norm_ps")
+        for b in range(4):
+            nc.tensor.transpose(norm_ps[:, b, :], norm4[:, b : b + 1].to_broadcast([P, P]), ident[:])
+        norm_all = held.tile([P, N], F32, name="norm_all")
+        nc.scalar.copy(norm_all[:].rearrange("p (n b) -> p n b", b=4), norm_ps[:].rearrange("p b n -> p n b"))
+
+        gathered = held.tile([P, 4, N], F32, name="gathered")
+        k_bf = [held.tile([P, w, 4], BF16, align_bytes=64, name=f"k_bf{s}") for s, (c0, w) in enumerate(SLICES)]
+
+        def gather(t, c0, w):
+            nc.vector.tensor_tensor(
+                gathered[:, t, c0 : c0 + w],
+                planes[t][:].indirect(offsets[:, c0 // 16 : (c0 + w) // 16]),
+                norm_all[:, c0 : c0 + w],
+                MULT,
+            )
+
+        def pair_copy(pair, s):
+            c0, w = SLICES[s]
+            nc.scalar.copy(
+                k_bf[s][:, :, 2 * pair : 2 * pair + 2],
+                gathered[:, 2 * pair : 2 * pair + 2, c0 : c0 + w].rearrange("p t n -> p n t"),
+            )
+
+        for t in range(3):
+            for c0 in (0, 256):
+                gather(t, c0, 256)
+        for s in range(4):
+            pair_copy(0, s)
+
+        q_bf = held.tile([P, NQ, 4], BF16, align_bytes=64, name="q_bf")
+        q_codes = held.tile([P, NQ], U32, align_bytes=64, name="q_codes")
+        q_scales = held.tile([P, NQ], U8, align_bytes=64, name="q_scales")
+        k_codes = [held.tile([P, w], U32, align_bytes=64, name=f"k_codes{s}") for s, (c0, w) in enumerate(SLICES)]
+        k_scales = [held.tile([P, w], U8, align_bytes=64, name=f"k_scales{s}") for s, (c0, w) in enumerate(SLICES)]
+        scores = [psum.tile([P, 2, w], F32, name=f"scores{s}") for s, (c0, w) in enumerate(SLICES)]
+        result = held.tile([P, 2, N // SEG], F32, name="result")
+
+        def q_cast():
+            for copy, cols in ((nc.vector.tensor_copy, slice(0, 192)), (nc.scalar.copy, slice(192, NQ))):
+                copy(q_bf[:, cols, :], q_raw[:, :, cols].rearrange("p t c -> p c t"))
+
+        def q_quantize():
+            nc.vector.quantize_mx(
+                out=q_codes[:].bitcast(FP8X4), scales=q_scales[:], in_=q_bf[:].rearrange("p c t -> p (c t)")
+            )
+
+        def k_quantize(s):
+            nc.vector.quantize_mx(
+                out=k_codes[s][:].bitcast(FP8X4), scales=k_scales[s][:], in_=k_bf[s][:].rearrange("p c t -> p (c t)")
+            )
+
+        def multiply(s):
+            for m in range(2):
+                nc.tensor.matmul_mx(
+                    out=scores[s][:, m, :],
+                    lhsT=q_codes[:, m * P : (m + 1) * P].bitcast(FP8X4),
+                    lhsT_scale=q_scales[:, m * P : (m + 1) * P],
+                    rhs=k_codes[s][:].bitcast(FP8X4),
+                    rhs_scale=k_scales[s][:],
+                    start=True,
+                    stop=True,
+                )
+
+        def maxima(s):
+            c0, w = SLICES[s]
+            nc.vector.tensor_reduce(
+                out=result[:, :, c0 // SEG : (c0 + w) // SEG],
+                in_=scores[s][:].rearrange("p m (j i) -> p m j i", i=SEG),
+                axis=AXIS_X,
+                op=MAX,
+            )
+
+        for s in range(4):
+            gather(3, *SLICES[s])
+        pair_copy(1, 0)
+        pair_copy(1, 1)
+        q_cast()
+        pair_copy(1, 2)
+        pair_copy(1, 3)
+        k_quantize(0)
+        q_quantize()
+        k_quantize(1)
+        k_quantize(2)
+        k_quantize(3)
+        for s in range(4):
+            multiply(s)
+        for s in range(4):
+            maxima(s)
+        nc.sync.dma_start(out[0].rearrange("(m p) j -> p m j", m=2), result[:])

@@ -42,7 +42,7 @@ def tile_attend_pq_max32_kernel(tc, qT, cb, norm, offs, out):
         ident = held.tile([P, P], F32, name="ident")
         make_identity(nc, ident[:])
 
-        norm_ps = psum.tile([P, 4, P], F32, name="norm_ps")
+        norm_ps = psum.tile([P, 4, P], F32, name="norm_ps", tag="bank7")
         for b in range(4):
             nc.tensor.transpose(norm_ps[:, b, :], norm4[:, b : b + 1].to_broadcast([P, P]), ident[:])
         norm_all = held.tile([P, N], F32, name="norm_all")
@@ -72,21 +72,23 @@ def tile_attend_pq_max32_kernel(tc, qT, cb, norm, offs, out):
         for s in range(4):
             pair_copy(0, s)
 
-        q_bf = held.tile([P, NQ, 4], BF16, align_bytes=64, name="q_bf")
-        q_codes = held.tile([P, NQ], U32, align_bytes=64, name="q_codes")
-        q_scales = held.tile([P, NQ], U8, align_bytes=64, name="q_scales")
+        q_bf = [held.tile([P, P, 4], BF16, align_bytes=64, name=f"q_bf{m}") for m in range(2)]
+        q_codes = [held.tile([P, P], U32, align_bytes=64, name=f"q_codes{m}") for m in range(2)]
+        q_scales = [held.tile([P, P], U8, align_bytes=64, name=f"q_scales{m}") for m in range(2)]
         k_codes = [held.tile([P, w], U32, align_bytes=64, name=f"k_codes{s}") for s, (c0, w) in enumerate(SLICES)]
         k_scales = [held.tile([P, w], U8, align_bytes=64, name=f"k_scales{s}") for s, (c0, w) in enumerate(SLICES)]
-        scores = [psum.tile([P, 2, w], F32, name=f"scores{s}") for s, (c0, w) in enumerate(SLICES)]
         result = held.tile([P, 2, N // SEG], F32, name="result")
+        scores = {}
 
-        def q_cast():
-            for copy, cols in ((nc.vector.tensor_copy, slice(0, 192)), (nc.scalar.copy, slice(192, NQ))):
-                copy(q_bf[:, cols, :], q_raw[:, :, cols].rearrange("p t c -> p c t"))
+        def q_cast(m, copy, g0, g1):
+            copy(
+                q_bf[m][:].rearrange("p (g r) t -> p g t r", r=2)[:, g0:g1],
+                q_raw[:].rearrange("p t (g r m) -> p m g t r", r=2, m=2)[:, m, g0:g1],
+            )
 
-        def q_quantize():
+        def q_quantize(m):
             nc.vector.quantize_mx(
-                out=q_codes[:].bitcast(FP8X4), scales=q_scales[:], in_=q_bf[:].rearrange("p c t -> p (c t)")
+                out=q_codes[m][:].bitcast(FP8X4), scales=q_scales[m][:], in_=q_bf[m][:].rearrange("p c t -> p (c t)")
             )
 
         def k_quantize(s):
@@ -94,23 +96,23 @@ def tile_attend_pq_max32_kernel(tc, qT, cb, norm, offs, out):
                 out=k_codes[s][:].bitcast(FP8X4), scales=k_scales[s][:], in_=k_bf[s][:].rearrange("p c t -> p (c t)")
             )
 
-        def multiply(s):
-            for m in range(2):
-                nc.tensor.matmul_mx(
-                    out=scores[s][:, m, :],
-                    lhsT=q_codes[:, m * P : (m + 1) * P].bitcast(FP8X4),
-                    lhsT_scale=q_scales[:, m * P : (m + 1) * P],
-                    rhs=k_codes[s][:].bitcast(FP8X4),
-                    rhs_scale=k_scales[s][:],
-                    start=True,
-                    stop=True,
-                )
+        def multiply(m, s):
+            scores[m, s] = psum.tile([P, SLICES[s][1]], F32, name=f"scores{m}{s}", tag=f"bank{2 * s + m}")
+            nc.tensor.matmul_mx(
+                out=scores[m, s][:],
+                lhsT=q_codes[m][:].bitcast(FP8X4),
+                lhsT_scale=q_scales[m][:],
+                rhs=k_codes[s][:].bitcast(FP8X4),
+                rhs_scale=k_scales[s][:],
+                start=True,
+                stop=True,
+            )
 
-        def maxima(s):
+        def maxima(m, s):
             c0, w = SLICES[s]
             nc.vector.tensor_reduce(
-                out=result[:, :, c0 // SEG : (c0 + w) // SEG],
-                in_=scores[s][:].rearrange("p m (j i) -> p m j i", i=SEG),
+                out=result[:, m, c0 // SEG : (c0 + w) // SEG],
+                in_=scores[m, s][:].rearrange("p (j i) -> p j i", i=SEG),
                 axis=AXIS_X,
                 op=MAX,
             )
@@ -119,16 +121,20 @@ def tile_attend_pq_max32_kernel(tc, qT, cb, norm, offs, out):
             gather(3, *SLICES[s])
         pair_copy(1, 0)
         pair_copy(1, 1)
-        q_cast()
+        q_cast(1, nc.scalar.copy, 44, 64)
         pair_copy(1, 2)
         pair_copy(1, 3)
+        q_cast(0, nc.vector.tensor_copy, 0, 64)
         k_quantize(0)
-        q_quantize()
+        q_cast(1, nc.vector.tensor_copy, 0, 44)
+        q_quantize(0)
         k_quantize(1)
+        q_quantize(1)
         k_quantize(2)
         k_quantize(3)
-        for s in range(4):
-            multiply(s)
-        for s in range(4):
-            maxima(s)
-        nc.sync.dma_start(out[0].rearrange("(m p) j -> p m j", m=2), result[:])
+        order = [(0, 0), (0, 1), (1, 0), (1, 1), (0, 2), (1, 2), (0, 3), (1, 3)]
+        for m, s in order:
+            multiply(m, s)
+        for m, s in order:
+            maxima(m, s)
+        nc.sync.dma_start(out[0].rearrange("(p m) j -> p m j", m=2), result[:])

@@ -121,12 +121,12 @@ def tile_attend_pq_max32_kernel(tc, qT, cb, norm, offs, out):
             gather(3, *SLICES[s])
         pair_copy(1, 0)
         pair_copy(1, 1)
-        q_cast(1, nc.scalar.copy, 44, 64)
+        q_cast(1, nc.scalar.copy, 32, 64)
         pair_copy(1, 2)
         pair_copy(1, 3)
         q_cast(0, nc.vector.tensor_copy, 0, 64)
         k_quantize(0)
-        q_cast(1, nc.vector.tensor_copy, 0, 44)
+        q_cast(1, nc.vector.tensor_copy, 0, 32)
         q_quantize(0)
         k_quantize(1)
         q_quantize(1)

@@ -117,16 +117,16 @@ def tile_attend_pq_max32_kernel(tc, qT, cb, norm, offs, out):
                 op=MAX,
             )
 
-        for s in range(4):
-            gather(3, *SLICES[s])
+        for c0, w in ((0, 128), (128, 128), (256, 256)):
+            gather(3, c0, w)
         pair_copy(1, 0)
         pair_copy(1, 1)
-        q_cast(1, nc.scalar.copy, 32, 64)
+        q_cast(1, nc.scalar.copy, 38, 64)
         pair_copy(1, 2)
         pair_copy(1, 3)
         q_cast(0, nc.vector.tensor_copy, 0, 64)
         k_quantize(0)
-        q_cast(1, nc.vector.tensor_copy, 0, 32)
+        q_cast(1, nc.vector.tensor_copy, 0, 38)
         q_quantize(0)
         k_quantize(1)
         q_quantize(1)

@@ -28,8 +28,8 @@ def tile_attend_pq_max32_kernel(tc, qT, cb, norm, offs, out):
 
         offsets = held.tile([P, N // 16], U16, name="offsets")
         norm4 = held.tile([P, 4], F32, name="norm4")
-        planes = [held.tile([P, C], F32, name=f"plane{t}") for t in range(4)]
-        q_raw = held.tile([P, 4, NQ], F32, name="q_raw")
+        planes = [held.tile([P, C], F32, align_bytes=256, name=f"plane{t}") for t in range(4)]
+        q_raw = held.tile([P, 4, NQ], F32, align_bytes=256, name="q_raw")
 
         cb_rows = cb.rearrange("(p t) c -> p t c", t=4)
         nc.sync.dma_start(planes[0][:], cb_rows[:, 0, :])
@@ -77,7 +77,7 @@ def tile_attend_pq_max32_kernel(tc, qT, cb, norm, offs, out):
         q_scales = [held.tile([P, P], U8, align_bytes=64, name=f"q_scales{m}") for m in range(2)]
         k_codes = [held.tile([P, w], U32, align_bytes=64, name=f"k_codes{s}") for s, (c0, w) in enumerate(SLICES)]
         k_scales = [held.tile([P, w], U8, align_bytes=64, name=f"k_scales{s}") for s, (c0, w) in enumerate(SLICES)]
-        result = held.tile([P, 2, N // SEG], F32, name="result")
+        result = held.tile([P, 2, N // SEG], F32, align_bytes=256, name="result")
         scores = {}
 
         def q_cast(m, copy, g0, g1):

@@ -26,10 +26,10 @@ def tile_attend_pq_max32_kernel(tc, qT, cb, norm, offs, out):
         held = ctx.enter_context(tc.tile_pool(name="held", bufs=1))
         psum = ctx.enter_context(tc.psum_pool(name="psum", bufs=1))
 
-        offsets = held.tile([P, N // 16], U16, name="offsets")
-        norm4 = held.tile([P, 4], F32, name="norm4")
-        planes = [held.tile([P, C], F32, align_bytes=256, name=f"plane{t}") for t in range(4)]
-        q_raw = held.tile([P, 4, NQ], F32, align_bytes=256, name="q_raw")
+        offsets = held.tile([P, N // 16], U16, align_bytes=256, name="offsets")
+        norm4 = held.tile([P, 4], F32, align_bytes=256, name="norm4")
+        planes = [held.tile([P, C], F32, align_bytes=4096, name=f"plane{t}") for t in range(4)]
+        q_raw = held.tile([P, 4, NQ], F32, align_bytes=4096, name="q_raw")
 
         cb_rows = cb.rearrange("(p t) c -> p t c", t=4)
         nc.sync.dma_start(planes[0][:], cb_rows[:, 0, :])

@@ -24,12 +24,14 @@ def tile_attend_pq_max32_kernel(tc, qT, cb, norm, offs, out):
     nc = tc.nc
     with ExitStack() as ctx:
         held = ctx.enter_context(tc.tile_pool(name="held", bufs=1))
+        far = ctx.enter_context(tc.tile_pool(name="far", bufs=1))
         psum = ctx.enter_context(tc.psum_pool(name="psum", bufs=1))
 
         offsets = held.tile([P, N // 16], U16, align_bytes=256, name="offsets")
         norm4 = held.tile([P, 4], F32, align_bytes=256, name="norm4")
-        planes = [held.tile([P, C], F32, align_bytes=4096, name=f"plane{t}") for t in range(4)]
-        q_raw = held.tile([P, 4, NQ], F32, align_bytes=4096, name="q_raw")
+        planes = [held.tile([P, C], F32, align_bytes=4096, name=f"plane{t}") for t in range(3)]
+        planes.append(far.tile([P, C], F32, align_bytes=4096, offset=32768, name="plane3"))
+        q_raw = far.tile([P, 4, NQ], F32, align_bytes=4096, offset=32768 + 65536, name="q_raw")
 
         cb_rows = cb.rearrange("(p t) c -> p t c", t=4)
         nc.sync.dma_start(planes[0][:], cb_rows[:, 0, :])
@@ -48,7 +50,7 @@ def tile_attend_pq_max32_kernel(tc, qT, cb, norm, offs, out):
         norm_all = held.tile([P, N], F32, name="norm_all")
         nc.scalar.copy(norm_all[:].rearrange("p (n b) -> p n b", b=4), norm_ps[:].rearrange("p b n -> p n b"))
 
-        gathered = held.tile([P, 4, N], F32, name="gathered")
+        gathered = far.tile([P, 4, N], F32, align_bytes=4096, offset=32768 + 2 * 65536, name="gathered")
         k_bf = [held.tile([P, w, 4], BF16, align_bytes=64, name=f"k_bf{s}") for s, (c0, w) in enumerate(SLICES)]
 
         def gather(t, c0, w):

from contextlib import ExitStack

import concourse.mybir as mybir
from concourse.masks import make_identity

F32 = mybir.dt.float32
BF16 = mybir.dt.bfloat16
U32 = mybir.dt.uint32
U16 = mybir.dt.uint16
U8 = mybir.dt.uint8
FP8X4 = mybir.dt.float8_e4m3fn_x4
MULT = mybir.AluOpType.mult
MAX = mybir.AluOpType.max
AXIS_X = mybir.AxisListType.X

D, C, N, NQ, SEG = 512, 2048, 512, 256, 32
P = 128
FLOPS = 2 * D * N * NQ

SLICES = ((0, 128), (128, 128), (256, 128), (384, 128))


def tile_attend_pq_max32_kernel(tc, qT, cb, norm, offs, out):
    nc = tc.nc
    with ExitStack() as ctx:
        held = ctx.enter_context(tc.tile_pool(name="held", bufs=1))
        far = ctx.enter_context(tc.tile_pool(name="far", bufs=1))
        psum = ctx.enter_context(tc.psum_pool(name="psum", bufs=1))

        offsets = held.tile([P, N // 16], U16, align_bytes=256, name="offsets")
        norm4 = held.tile([P, 4], F32, align_bytes=256, name="norm4")
        planes = [held.tile([P, C], F32, align_bytes=4096, name=f"plane{t}") for t in range(3)]
        planes.append(far.tile([P, C], F32, align_bytes=4096, offset=32768, name="plane3"))
        q_raw = far.tile([P, 4, NQ], F32, align_bytes=4096, offset=32768 + 65536, name="q_raw")

        cb_rows = cb.rearrange("(p t) c -> p t c", t=4)
        nc.sync.dma_start(planes[0][:], cb_rows[:, 0, :])
        nc.sync.dma_start(norm4[:], norm[0:1, :].rearrange("o (p b) -> (o p) b", b=4))
        nc.sync.dma_start(offsets[:], offs)
        for t in range(1, 4):
            nc.sync.dma_start(planes[t][:], cb_rows[:, t, :])
        nc.sync.dma_start(q_raw[:], qT[0].rearrange("(p t) q -> p t q", t=4))

        ident = held.tile([P, P], F32, name="ident")
        make_identity(nc, ident[:])

        norm_ps = psum.tile([P, 4, P], F32, name="norm_ps", tag="bank7")
        for b in range(4):
            nc.tensor.transpose(norm_ps[:, b, :], norm4[:, b : b + 1].to_broadcast([P, P]), ident[:])
        norm_all = held.tile([P, N], F32, name="norm_all")
        nc.scalar.copy(norm_all[:].rearrange("p (n b) -> p n b", b=4), norm_ps[:].rearrange("p b n -> p n b"))

        gathered = far.tile([P, 4, N], F32, align_bytes=4096, offset=32768 + 2 * 65536, name="gathered")
        k_bf = [held.tile([P, w, 4], BF16, align_bytes=64, name=f"k_bf{s}") for s, (c0, w) in enumerate(SLICES)]

        def gather(t, c0, w):
            nc.vector.tensor_tensor(
                gathered[:, t, c0 : c0 + w],
                planes[t][:].indirect(offsets[:, c0 // 16 : (c0 + w) // 16]),
                norm_all[:, c0 : c0 + w],
                MULT,
            )

        def pair_copy(pair, s):
            c0, w = SLICES[s]
            nc.scalar.copy(
                k_bf[s][:, :, 2 * pair : 2 * pair + 2],
                gathered[:, 2 * pair : 2 * pair + 2, c0 : c0 + w].rearrange("p t n -> p n t"),
            )

        for t in range(3):
            for c0 in (0, 256):
                gather(t, c0, 256)
        for s in range(4):
            pair_copy(0, s)

        q_bf = [held.tile([P, P, 4], BF16, align_bytes=64, name=f"q_bf{m}") for m in range(2)]
        q_codes = [held.tile([P, P], U32, align_bytes=64, name=f"q_codes{m}") for m in range(2)]
        q_scales = [held.tile([P, P], U8, align_bytes=64, name=f"q_scales{m}") for m in range(2)]
        k_codes = [held.tile([P, w], U32, align_bytes=64, name=f"k_codes{s}") for s, (c0, w) in enumerate(SLICES)]
        k_scales = [held.tile([P, w], U8, align_bytes=64, name=f"k_scales{s}") for s, (c0, w) in enumerate(SLICES)]
        result = held.tile([P, 2, N // SEG], F32, align_bytes=256, name="result")
        scores = {}

        def q_cast(m, copy, g0, g1):
            copy(
                q_bf[m][:].rearrange("p (g r) t -> p g t r", r=2)[:, g0:g1],
                q_raw[:].rearrange("p t (g r m) -> p m g t r", r=2, m=2)[:, m, g0:g1],
            )

        def q_quantize(m):
            nc.vector.quantize_mx(
                out=q_codes[m][:].bitcast(FP8X4), scales=q_scales[m][:], in_=q_bf[m][:].rearrange("p c t -> p (c t)")
            )

        def k_quantize(s):
            nc.vector.quantize_mx(
                out=k_codes[s][:].bitcast(FP8X4), scales=k_scales[s][:], in_=k_bf[s][:].rearrange("p c t -> p (c t)")
            )

        def multiply(m, s):
            scores[m, s] = psum.tile([P, SLICES[s][1]], F32, name=f"scores{m}{s}", tag=f"bank{2 * s + m}")
            nc.tensor.matmul_mx(
                out=scores[m, s][:],
                lhsT=q_codes[m][:].bitcast(FP8X4),
                lhsT_scale=q_scales[m][:],
                rhs=k_codes[s][:].bitcast(FP8X4),
                rhs_scale=k_scales[s][:],
                start=True,
                stop=True,
            )

        def maxima(m, s):
            c0, w = SLICES[s]
            nc.vector.tensor_reduce(
                out=result[:, m, c0 // SEG : (c0 + w) // SEG],
                in_=scores[m, s][:].rearrange("p (j i) -> p j i", i=SEG),
                axis=AXIS_X,
                op=MAX,
            )

        for c0, w in ((0, 128), (128, 128), (256, 256)):
            gather(3, c0, w)
        pair_copy(1, 0)
        pair_copy(1, 1)
        q_cast(1, nc.scalar.copy, 38, 64)
        pair_copy(1, 2)
        pair_copy(1, 3)
        q_cast(0, nc.vector.tensor_copy, 0, 64)
        k_quantize(0)
        q_cast(1, nc.vector.tensor_copy, 0, 38)
        q_quantize(0)
        k_quantize(1)
        q_quantize(1)
        k_quantize(2)
        k_quantize(3)
        order = [(0, 0), (0, 1), (1, 0), (1, 1), (0, 2), (1, 2), (0, 3), (1, 3)]
        for m, s in order:
            multiply(m, s)
        for m, s in order:
            maxima(m, s)
        nc.sync.dma_start(out[0].rearrange("(p m) j -> p m j", m=2), result[:])
